import numpy as np
import ml_dtypes


def mxq(x, axis, fmt="e4m3"):
    dtype, down = {"e4m3": (ml_dtypes.float8_e4m3fn, 7), "e5m2": (ml_dtypes.float8_e5m2, 14)}[fmt]
    v = np.moveaxis(np.asarray(x, np.float32).astype(ml_dtypes.bfloat16).astype(np.float64), axis, -1)
    blocks = v.reshape(v.shape[:-1] + (-1, 32))
    amax = np.abs(blocks).max(-1, keepdims=True)
    byte = np.maximum(np.where(amax > 0, np.frexp(amax)[1] - 1 + 127, 0) - down, 1)
    scale = np.exp2(byte - 127.0)
    codes = (blocks / scale).astype(np.float32).astype(dtype).astype(np.float64)
    return np.moveaxis((codes * scale).reshape(v.shape), -1, axis)


WIDE = False


def mx_kscale(k):
    if not WIDE:
        return np.ones(k)
    levels = np.array([10, -10, 5, -5, 0])
    if k % 512:
        return np.exp2(np.random.permutation(np.resize(levels, k // 32))).repeat(32)
    a = np.empty((k // 512, 16))
    for p in range(k // 512):
        a[p, :8] = np.random.permutation(np.resize(levels, 8))
        for g in range(8):
            far = levels[np.abs(levels - a[p, g]) >= 10]
            a[p, g + 8] = far[np.random.randint(len(far))]
    return np.exp2(a.ravel()).repeat(32)


def f64(x):
    return np.asarray(x).astype(np.float64)


def striped(idx):
    return np.tile(idx.reshape(-1, 16).T, (8, 1)).astype(np.uint16)


def unstriped(offs):
    return offs[:16].T.reshape(-1).astype(np.int64)


E2M1 = np.array([0.0, 0.5, 1.0, 1.5, 2.0, 3.0, 4.0, 6.0, -0.0, -0.5, -1.0, -1.5, -2.0, -3.0, -4.0, -6.0])


def pack_weight(w, fmt):
    k, n = w.shape
    w = f64(np.asarray(w, np.float32).astype(ml_dtypes.bfloat16)).reshape(k // 32, 32, n)
    amax = np.abs(w).max(1)
    if fmt == "e4m3":
        byte = np.frexp(amax)[1] - 1 + 127 - 7
    else:
        mant, ex = np.frexp(amax / 6.0)
        byte = np.where(mant > 0.5, ex, ex - 1) + 127
    byte = np.clip(np.where(amax > 0, byte, 1), 1, 254)
    scaled = (w * np.exp2(127.0 - byte)[:, None, :]).reshape(k, n).astype(np.float32)
    by_word = np.ascontiguousarray(scaled.reshape(k // 512, 128, 4, n).transpose(0, 1, 3, 2))
    if fmt == "e4m3":
        words = by_word.astype(ml_dtypes.float8_e4m3fn).view(np.uint8)
    else:
        c = by_word.astype(ml_dtypes.float4_e2m1fn).view(np.uint8) & 0xF
        words = (c[..., 0::2] | (c[..., 1::2] << 4)).reshape(k // 512, 128, 2 * n)
    return np.ascontiguousarray(words), np.ascontiguousarray(byte.astype(np.uint8).reshape(k // 512, 16, n))


def unpack_weight(words, scales, fmt):
    g, _, n = scales.shape
    words = np.ascontiguousarray(words).reshape(g, 128, n, -1)
    if fmt == "e4m3":
        vals = words.view(ml_dtypes.float8_e4m3fn).astype(np.float64)
    else:
        nib = np.empty((g, 128, n, 4), np.uint8)
        nib[..., 0::2] = words & 0xF
        nib[..., 1::2] = words >> 4
        vals = E2M1[nib]
    vals = vals * np.repeat(np.exp2(scales.astype(np.float64) - 127.0), 8, axis=1)[..., None]
    return vals.transpose(0, 1, 3, 2).reshape(g * 512, n)


def gelu(v):
    return 0.5 * v * (1.0 + np.tanh(np.sqrt(2.0 / np.pi) * (v + 0.044715 * v**3)))


K, T, E, C, H, N = 512, 1024, 4, 128, 512, 128


def by_expert(wq, xq):
    return np.concatenate([wq[e].T @ xq[:, e * C:(e + 1) * C] for e in range(E)], axis=1)


def setup_inputs():
    n = np.random.standard_normal
    s = mx_kscale(K)[:, None]
    u = mx_kscale(H)
    x = pack_weight(n((K, T)) * s, "e4m3")
    return {
        "x_words": x[0],
        "x_scales": x[1],
        "w1": (n((E + 1, K, H)) / np.sqrt(K) / s[None]).astype(np.float32),
        "w3": (n((E + 1, K, H)) / np.sqrt(K) / s[None] * u[None, None, :]).astype(np.float32),
        "w2": (n((E + 1, H, N)) / np.sqrt(H) / u[None, :, None]).astype(np.float32),
        "gate": np.tile(np.random.uniform(0.2, 1.0, E * C), (N, 1)).astype(np.float32),
        "offs": striped(np.random.permutation(T)[:E * C]),
    }


def reference(x_words, x_scales, w1, w3, w2, gate, offs):
    idx = unstriped(offs)
    w1q, w3q, w2q = mxq(f64(w1), 1, "e4m3"), mxq(f64(w3), 1, "e4m3"), mxq(f64(w2), 1, "e4m3")
    xs = unpack_weight(x_words, x_scales, "e4m3")
    hs = gelu(w1q[E].T @ xs) * (w3q[E].T @ xs)
    ys = w2q[E].T @ mxq(hs, 0, "e4m3")
    xq = unpack_weight(x_words, x_scales, "e4m3")[:, idx]
    h = gelu(by_expert(w1q, xq))
    h = h * by_expert(w3q, xq)
    y = by_expert(w2q, mxq(h, 0, "e4m3"))
    out = ys
    out[:, idx] += f64(gate) * y
    return out

@@ -1,0 +1,152 @@
+from contextlib import ExitStack
+
+import concourse.mybir as mybir
+
+K, T, E, C, H, N = 512, 1024, 4, 128, 512, 128
+SLOTS = E * C
+SHARED = E
+
+FLOPS = 2 * (T + SLOTS) * (2 * K * H + H * N)
+
+F32 = mybir.dt.float32
+BF16 = mybir.dt.bfloat16
+I32 = mybir.dt.int32
+U32 = mybir.dt.uint32
+U16 = mybir.dt.uint16
+U8 = mybir.dt.uint8
+FP8X4 = mybir.dt.float8_e4m3fn_x4
+GELU = mybir.ActivationFunctionType.Gelu_apprx_tanh
+MULT = mybir.AluOpType.mult
+ADD = mybir.AluOpType.add
+
+P = 128
+PACK = 4
+CHUNK = 128
+HALF = 512
+BANKS = {"e": 1, "s": 2}
+SCALAR_M = 80
+SCALAR_M_LAST = 44
+
+
+def tile_moe_shr_glu_gelu_kernel(tc, x_words, x_scales, w1, w3, w2, gate, offs, out):
+    nc = tc.nc
+    with ExitStack() as ctx:
+        keep = ctx.enter_context(tc.tile_pool(name="keep", bufs=1))
+        ring = ctx.enter_context(tc.tile_pool(name="ring", bufs=4))
+        psum = ctx.enter_context(tc.psum_pool(name="psum", bufs=1))
+
+        offsets = keep.tile([P, SLOTS // 16], U16, name="offsets")
+        words = keep.tile([P, T], I32, name="words", align_bytes=64)
+        planes = keep.tile([P, T // 4], I32, name="planes", align_bytes=64)
+        gates = keep.tile([P, SLOTS], F32, name="gates")
+        routed = keep.tile([P, T], F32, name="routed")
+        nc.vector.memset(planes[:], 0)
+        nc.vector.memset(routed[:], 0.0)
+
+        def load_up(name, w, cols):
+            raw = keep.tile([P, PACK, cols.stop - cols.start], F32, name=name)
+            nc.sync.dma_start(out=raw[:], in_=w.rearrange("(p j) c -> p j c", j=PACK)[:, :, cols])
+            return raw
+
+        def load_down(e):
+            raw = keep.tile([P, PACK, N], F32, name="raw2_%d" % e)
+            nc.sync.dma_start(out=raw[:], in_=w2[e].rearrange("(p j) n -> p j n", j=PACK))
+            return raw
+
+        whole = slice(0, H)
+        raw1, raw3, raw2 = {}, {}, {}
+        first = [load_up("raw1_s%d" % i, w1[SHARED], slice(256 * i, 256 * (i + 1))) for i in range(2)]
+        for q in range(4):
+            nc.scalar.dma_start(out=planes[32 * q : 32 * q + 4, :], in_=x_scales[0, 4 * q : 4 * q + 4, :].bitcast(I32))
+        nc.sync.dma_start(out=words[:], in_=x_words[0].rearrange("p t r -> p (t r)").bitcast(I32))
+        nc.sync.dma_start(offsets[:], offs)
+        raw3[SHARED] = load_up("raw3_s", w3[SHARED], whole)
+        for e in range(E):
+            raw1[e] = load_up("raw1_%d" % e, w1[e], whole)
+            raw3[e] = load_up("raw3_%d" % e, w3[e], whole)
+            if e < 2:
+                raw2[e] = load_down(e)
+            if e == 0:
+                nc.sync.dma_start(out=gates[:], in_=gate)
+        for e in (2, 3, SHARED):
+            raw2[e] = load_down(e)
+
+        def quantize(name, staged, width):
+            codes = keep.tile([P, width], U32, name="codes_" + name, align_bytes=64)
+            scales = keep.tile([P, width], U8, name="scales_" + name, align_bytes=64)
+            nc.vector.quantize_mx(out=codes[:].bitcast(FP8X4), scales=scales[:], in_=staged)
+            return codes, scales
+
+        def quantize_up(name, scalar_src, vector_src, split):
+            staged = ring.tile([P, 2, 2, P, PACK], BF16, name="staged_up", align_bytes=64)
+            order = "p u t m j -> p u m j t"
+            nc.scalar.copy(out=staged[:, :, :, 0:split, :].rearrange(order), in_=scalar_src.rearrange("p j (m u t) -> p u m j t", u=2, t=2))
+            nc.vector.tensor_copy(out=staged[:, :, :, split:P, :].rearrange(order), in_=vector_src.rearrange("p j (m u t) -> p u m j t", u=2, t=2))
+            return quantize(name, staged[:].rearrange("p u t m j -> p (u t m j)"), H)
+
+        def quantize_whole(name, raw, split):
+            return quantize_up(name, raw[:, :, 0 : PACK * split], raw[:, :, PACK * split : H], split)
+
+        def quantize_down(e):
+            staged = ring.tile([P, N // 4, 4, PACK], BF16, name="staged_down", align_bytes=64)
+            nc.scalar.copy(out=staged[:].rearrange("p c i j -> p c j i"), in_=raw2[e][:].rearrange("p j (c i) -> p c j i", i=4))
+            return quantize("w2_%d" % e, staged[:].rearrange("p c i j -> p (c i j)"), N)
+
+        def up(tag, bufs, weights, x_codes, x_planes):
+            codes, scales = weights
+            bank = psum.tile([P, PACK, CHUNK], F32, name=tag, bufs=bufs)
+            for t in range(PACK):
+                cols = slice(P * t, P * (t + 1))
+                nc.tensor.matmul_mx(out=bank[:, t, :], lhsT=codes[:, cols].bitcast(FP8X4), lhsT_scale=scales[:, cols],
+                                    rhs=x_codes.bitcast(FP8X4), rhs_scale=x_planes, start=True, stop=True)
+            return bank[:].rearrange("p t n -> p n t")
+
+        def activate(name, kind, weights, x_codes, x_planes):
+            act = keep.tile([P, CHUNK, PACK], F32, name="act_" + name)
+            nc.scalar.activation(out=act[:], in_=up("a1" + kind, BANKS[kind], weights, x_codes, x_planes), func=GELU)
+            return act
+
+        def gated(hidden, kind, act, weights, x_codes, x_planes):
+            nc.vector.tensor_tensor(out=hidden, in0=up("a3" + kind, BANKS[kind], weights, x_codes, x_planes), in1=act[:], op=MULT)
+
+        def down(weights, hidden, width):
+            bank = psum.tile([P, HALF], F32, name="y", bufs=2)
+            nc.tensor.matmul_mx(out=bank[:, 0:width], lhsT=weights[0][:].bitcast(FP8X4), lhsT_scale=weights[1][:],
+                                rhs=hidden[0][:].bitcast(FP8X4), rhs_scale=hidden[1][:], start=True, stop=True)
+            return bank[:, 0:width]
+
+        plane_bytes = planes[:].bitcast(U8)
+        q1s = quantize_up("w1_s", first[0][:], first[1][:], P // 2)
+        q3s = quantize_whole("w3_s", raw3[SHARED], SCALAR_M)
+
+        slot_words = keep.tile([P, SLOTS], U32, name="slot_words", align_bytes=64)
+        slot_planes = keep.tile([P, SLOTS], U8, name="slot_planes", align_bytes=64)
+        nc.vector.tensor_copy(slot_words[:], words[:].bitcast(U32).indirect(offsets[:]))
+        nc.vector.tensor_copy(slot_planes[:], plane_bytes.indirect(offsets[:]))
+
+        for e in range(E):
+            slots = slice(C * e, C * (e + 1))
+            q1 = quantize_whole("w1_%d" % e, raw1[e], SCALAR_M)
+            act = activate("e%d" % e, "e", q1, slot_words[:, slots], slot_planes[:, slots])
+            q3 = quantize_whole("w3_%d" % e, raw3[e], SCALAR_M_LAST if e == E - 1 else SCALAR_M)
+            hidden = keep.tile([P, C, PACK], BF16, name="hidden_e%d" % e, align_bytes=64)
+            gated(hidden[:], "e", act, q3, slot_words[:, slots], slot_planes[:, slots])
+            hq = quantize("h_e%d" % e, hidden[:].rearrange("p n t -> p (n t)"), C)
+            q2 = quantize_down(e)
+            y = keep.tile([P, C], F32, name="y_e%d" % e)
+            nc.scalar.copy(out=y[:], in_=down(q2, hq, C))
+            nc.vector.tensor_tensor(routed[:].indirect(offsets[:, 8 * e : 8 * (e + 1)]), y[:], gates[:, slots], MULT)
+
+        q2s = quantize_down(SHARED)
+        for half in range(T // HALF):
+            hidden = keep.tile([P, HALF, PACK], BF16, name="hidden_s%d" % half, align_bytes=64)
+            for i in range(HALF // CHUNK):
+                start = HALF * half + CHUNK * i
+                tokens = slice(start, start + CHUNK)
+                act = activate("s%d" % start, "s", q1s, words[:, tokens], plane_bytes[:, tokens])
+                gated(hidden[:, CHUNK * i : CHUNK * (i + 1), :], "s", act, q3s, words[:, tokens], plane_bytes[:, tokens])
+            hq = quantize("h_s%d" % half, hidden[:].rearrange("p n t -> p (n t)"), HALF)
+            tokens = slice(HALF * half, HALF * (half + 1))
+            result = keep.tile([P, HALF], F32, name="result%d" % half)
+            nc.vector.tensor_tensor(out=result[:], in0=down(q2s, hq, HALF), in1=routed[:, tokens], op=ADD)
+            nc.sync.dma_start(out=out[:, tokens], in_=result[:])

@@ -23,9 +23,11 @@ P = 128
 PACK = 4
 CHUNK = 128
 HALF = 512
-BANKS = {"e": 1, "s": 2}
-SCALAR_M = 80
-SCALAR_M_LAST = 44
+LOADS = ["w1sa","w1sb","w11","offs","x","w3s","w10","w30","w31","w12","w21","w32","gate","w13","w33b","w33a","w20","w22","w23","w2s"]
+SPLIT = {"w1s":64,"w3s":0,"w10":16,"w30":112,"w11":112,"w31":80,"w12":88,"w32":128,"w13":88,"w33":64}
+DOWN_ON = {"0":"S","1":"S","2":"S","3":"V","s":"S"}
+ORDER = ["cS_w11","gw","cV_w1s","cS_w1s","cS_w31","cV_w3s","q_w1s","gs","cV_w11","q_w11","cV_w31","cV_w30","q_w31","m1s5","gs5","m1s2","cV_w10","cS_w30","gs2","m1s1","q_w3s","cS_w10","m1s0","c_w22","q_w30","m3s5","hs5","c_w21","m3s2","m1s3","gs0","cS_w13","gs1","hs2","cV_w13","cS_w12","q_w10","m3s0","m3s1","q_w13","gs3","m1s7","q_w22","hs0","c_w23","m1s6","c_w20","cS_w33","cV_w12","c_w2s","q_w12","m11","cV_w33","gs7","m10","g1","hs1","m3s3","q_w23","m31","gs6","h1","m3s7","hs3","hs7","cS_w32","qh1","m30","m12","m3s6","q_w20","m3s4","g0","hs6","q_w21","m21","q_w33","m13","g3","h0","g2","qh0","m1s4","q_w32","gs4","m33","h3","qhs0","y1","m20","m32","h2","hs4","qh3","sc1","y0","qh2","m22","sc0","m23","q_w2s","y2","sc2","y3","sc3","qhs1","m2s1","m2s0","add0","add1"]
+GROUP = 4
 
 
 def tile_moe_shr_glu_gelu_kernel(tc, x_words, x_scales, w1, w3, w2, gate, offs, out):
@@ -40,113 +42,126 @@ def tile_moe_shr_glu_gelu_kernel(tc, x_words, x_scales, w1, w3, w2, gate, offs, 
         planes = keep.tile([P, T // 4], I32, name="planes", align_bytes=64)
         gates = keep.tile([P, SLOTS], F32, name="gates")
         routed = keep.tile([P, T], F32, name="routed")
+        slot_words = keep.tile([P, SLOTS], U32, name="slot_words", align_bytes=64)
+        slot_planes = keep.tile([P, SLOTS], U8, name="slot_planes", align_bytes=64)
+        plane_bytes = planes[:].bitcast(U8)
         nc.vector.memset(planes[:], 0)
         nc.vector.memset(routed[:], 0.0)
+        warm = keep.tile([P, 2], F32, name="warm")
+        nc.vector.memset(warm[:, 0:1], 0.0)
+        nc.scalar.activation(out=warm[:, 1:2], in_=warm[:, 0:1], func=GELU)
 
-        def load_up(name, w, cols):
-            raw = keep.tile([P, PACK, cols.stop - cols.start], F32, name=name)
-            nc.sync.dma_start(out=raw[:], in_=w.rearrange("(p j) c -> p j c", j=PACK)[:, :, cols])
-            return raw
-
-        def load_down(e):
-            raw = keep.tile([P, PACK, N], F32, name="raw2_%d" % e)
-            nc.sync.dma_start(out=raw[:], in_=w2[e].rearrange("(p j) n -> p j n", j=PACK))
-            return raw
-
-        whole = slice(0, H)
-        raw1, raw3, raw2 = {}, {}, {}
-        first = [load_up("raw1_s%d" % i, w1[SHARED], slice(256 * i, 256 * (i + 1))) for i in range(2)]
         for q in range(4):
             nc.scalar.dma_start(out=planes[32 * q : 32 * q + 4, :], in_=x_scales[0, 4 * q : 4 * q + 4, :].bitcast(I32))
-        nc.sync.dma_start(out=words[:], in_=x_words[0].rearrange("p t r -> p (t r)").bitcast(I32))
-        nc.sync.dma_start(offsets[:], offs)
-        raw3[SHARED] = load_up("raw3_s", w3[SHARED], whole)
-        for e in range(E):
-            raw1[e] = load_up("raw1_%d" % e, w1[e], whole)
-            raw3[e] = load_up("raw3_%d" % e, w3[e], whole)
-            if e < 2:
-                raw2[e] = load_down(e)
-            if e == 0:
+        raw = {}
+        mats = {"w1": w1, "w3": w3, "w2": w2}
+        for name in LOADS:
+            if name == "x":
+                nc.sync.dma_start(out=words[:], in_=x_words[0].rearrange("p t r -> p (t r)").bitcast(I32))
+            elif name == "offs":
+                nc.sync.dma_start(offsets[:], offs)
+            elif name == "gate":
                 nc.sync.dma_start(out=gates[:], in_=gate)
-        for e in (2, 3, SHARED):
-            raw2[e] = load_down(e)
+            else:
+                src = mats[name[:2]]["0123s".index(name[2])].rearrange("(p j) c -> p j c", j=PACK)
+                if len(name) == 4:
+                    src = src[:, :, 0:256] if name[3] == "a" else src[:, :, 256:512]
+                raw[name] = keep.tile(list(src.shape), F32, name="raw_" + name)
+                nc.sync.dma_start(out=raw[name][:], in_=src)
 
-        def quantize(name, staged, width):
+        staged, quant, banks, acts, hidden, ys = {}, {}, {}, {}, {}, {}
+
+        def quantize(name, src, width):
             codes = keep.tile([P, width], U32, name="codes_" + name, align_bytes=64)
             scales = keep.tile([P, width], U8, name="scales_" + name, align_bytes=64)
-            nc.vector.quantize_mx(out=codes[:].bitcast(FP8X4), scales=scales[:], in_=staged)
-            return codes, scales
+            nc.vector.quantize_mx(out=codes[:].bitcast(FP8X4), scales=scales[:], in_=src)
+            quant[name] = (codes, scales)
 
-        def quantize_up(name, scalar_src, vector_src, split):
-            staged = ring.tile([P, 2, 2, P, PACK], BF16, name="staged_up", align_bytes=64)
-            order = "p u t m j -> p u m j t"
-            nc.scalar.copy(out=staged[:, :, :, 0:split, :].rearrange(order), in_=scalar_src.rearrange("p j (m u t) -> p u m j t", u=2, t=2))
-            nc.vector.tensor_copy(out=staged[:, :, :, split:P, :].rearrange(order), in_=vector_src.rearrange("p j (m u t) -> p u m j t", u=2, t=2))
-            return quantize(name, staged[:].rearrange("p u t m j -> p (u t m j)"), H)
+        def cast_up(name, on_scalar):
+            if name not in staged:
+                staged[name] = ring.tile([P, 2, 2, P, PACK], BF16, name="staged_up", align_bytes=64)
+            split = SPLIT[name]
+            if name in raw:
+                src = raw[name][:, :, 0 : PACK * split] if on_scalar else raw[name][:, :, PACK * split : H]
+            else:
+                src = raw[name + ("a" if on_scalar else "b")][:]
+            dst = staged[name][:, :, :, 0:split, :] if on_scalar else staged[name][:, :, :, split:P, :]
+            copy = nc.scalar.copy if on_scalar else nc.vector.tensor_copy
+            copy(out=dst.rearrange("p u t m j -> p u m j t"), in_=src.rearrange("p j (m u t) -> p u m j t", u=2, t=2))
 
-        def quantize_whole(name, raw, split):
-            return quantize_up(name, raw[:, :, 0 : PACK * split], raw[:, :, PACK * split : H], split)
+        def cast_down(name):
+            staged[name] = ring.tile([P, N // 4, 4, PACK], BF16, name="staged_down", align_bytes=64)
+            copy = nc.scalar.copy if DOWN_ON[name[2]] == "S" else nc.vector.tensor_copy
+            copy(out=staged[name][:].rearrange("p c i j -> p c j i"), in_=raw[name][:].rearrange("p j (c i) -> p c j i", i=4))
 
-        def quantize_down(e):
-            staged = ring.tile([P, N // 4, 4, PACK], BF16, name="staged_down", align_bytes=64)
-            nc.scalar.copy(out=staged[:].rearrange("p c i j -> p c j i"), in_=raw2[e][:].rearrange("p j (c i) -> p c j i", i=4))
-            return quantize("w2_%d" % e, staged[:].rearrange("p c i j -> p (c i j)"), N)
-
-        def up(tag, bufs, weights, x_codes, x_planes):
-            codes, scales = weights
-            bank = psum.tile([P, PACK, CHUNK], F32, name=tag, bufs=bufs)
+        def up(which, unit):
+            codes, scales = quant["w" + which + unit[0]]
+            if unit[0] == "s":
+                tokens = slice(CHUNK * int(unit[1]), CHUNK * (int(unit[1]) + 1))
+                x_codes, x_planes = words[:, tokens], plane_bytes[:, tokens]
+            else:
+                tokens = slice(C * int(unit), C * (int(unit) + 1))
+                x_codes, x_planes = slot_words[:, tokens], slot_planes[:, tokens]
+            bank = psum.tile([P, PACK, CHUNK], F32, name="a" + which, bufs=3)
             for t in range(PACK):
                 cols = slice(P * t, P * (t + 1))
                 nc.tensor.matmul_mx(out=bank[:, t, :], lhsT=codes[:, cols].bitcast(FP8X4), lhsT_scale=scales[:, cols],
                                     rhs=x_codes.bitcast(FP8X4), rhs_scale=x_planes, start=True, stop=True)
-            return bank[:].rearrange("p t n -> p n t")
+            banks[which + unit] = bank[:].rearrange("p t n -> p n t")
 
-        def activate(name, kind, weights, x_codes, x_planes):
-            act = keep.tile([P, CHUNK, PACK], F32, name="act_" + name)
-            nc.scalar.activation(out=act[:], in_=up("a1" + kind, BANKS[kind], weights, x_codes, x_planes), func=GELU)
-            return act
+        def activate(unit):
+            acts[unit] = keep.tile([P, CHUNK, PACK], F32, name="act_" + unit)
+            nc.scalar.activation(out=acts[unit][:], in_=banks["1" + unit], func=GELU)
 
-        def gated(hidden, kind, act, weights, x_codes, x_planes):
-            nc.vector.tensor_tensor(out=hidden, in0=up("a3" + kind, BANKS[kind], weights, x_codes, x_planes), in1=act[:], op=MULT)
+        def gated(unit):
+            if unit[0] == "s":
+                group, place = divmod(int(unit[1]), GROUP)
+                key, width = "s%d" % group, GROUP * CHUNK
+            else:
+                key, place, width = unit, 0, C
+            if key not in hidden:
+                hidden[key] = keep.tile([P, width, PACK], BF16, name="hidden_" + key, align_bytes=64)
+            nc.vector.tensor_tensor(out=hidden[key][:, CHUNK * place : CHUNK * (place + 1), :], in0=banks["3" + unit], in1=acts[unit][:], op=MULT)
 
-        def down(weights, hidden, width):
+        def down(key):
+            width = GROUP * CHUNK if key[0] == "s" else C
             bank = psum.tile([P, HALF], F32, name="y", bufs=2)
-            nc.tensor.matmul_mx(out=bank[:, 0:width], lhsT=weights[0][:].bitcast(FP8X4), lhsT_scale=weights[1][:],
-                                rhs=hidden[0][:].bitcast(FP8X4), rhs_scale=hidden[1][:], start=True, stop=True)
-            return bank[:, 0:width]
+            wq, hq = quant["w2" + key[0]], quant["h" + key]
+            nc.tensor.matmul_mx(out=bank[:, 0:width], lhsT=wq[0][:].bitcast(FP8X4), lhsT_scale=wq[1][:],
+                                rhs=hq[0][:].bitcast(FP8X4), rhs_scale=hq[1][:], start=True, stop=True)
+            banks["2" + key] = bank[:, 0:width]
 
-        plane_bytes = planes[:].bitcast(U8)
-        q1s = quantize_up("w1_s", first[0][:], first[1][:], P // 2)
-        q3s = quantize_whole("w3_s", raw3[SHARED], SCALAR_M)
-
-        slot_words = keep.tile([P, SLOTS], U32, name="slot_words", align_bytes=64)
-        slot_planes = keep.tile([P, SLOTS], U8, name="slot_planes", align_bytes=64)
-        nc.vector.tensor_copy(slot_words[:], words[:].bitcast(U32).indirect(offsets[:]))
-        nc.vector.tensor_copy(slot_planes[:], plane_bytes.indirect(offsets[:]))
-
-        for e in range(E):
-            slots = slice(C * e, C * (e + 1))
-            q1 = quantize_whole("w1_%d" % e, raw1[e], SCALAR_M)
-            act = activate("e%d" % e, "e", q1, slot_words[:, slots], slot_planes[:, slots])
-            q3 = quantize_whole("w3_%d" % e, raw3[e], SCALAR_M_LAST if e == E - 1 else SCALAR_M)
-            hidden = keep.tile([P, C, PACK], BF16, name="hidden_e%d" % e, align_bytes=64)
-            gated(hidden[:], "e", act, q3, slot_words[:, slots], slot_planes[:, slots])
-            hq = quantize("h_e%d" % e, hidden[:].rearrange("p n t -> p (n t)"), C)
-            q2 = quantize_down(e)
-            y = keep.tile([P, C], F32, name="y_e%d" % e)
-            nc.scalar.copy(out=y[:], in_=down(q2, hq, C))
-            nc.vector.tensor_tensor(routed[:].indirect(offsets[:, 8 * e : 8 * (e + 1)]), y[:], gates[:, slots], MULT)
-
-        q2s = quantize_down(SHARED)
-        for half in range(T // HALF):
-            hidden = keep.tile([P, HALF, PACK], BF16, name="hidden_s%d" % half, align_bytes=64)
-            for i in range(HALF // CHUNK):
-                start = HALF * half + CHUNK * i
-                tokens = slice(start, start + CHUNK)
-                act = activate("s%d" % start, "s", q1s, words[:, tokens], plane_bytes[:, tokens])
-                gated(hidden[:, CHUNK * i : CHUNK * (i + 1), :], "s", act, q3s, words[:, tokens], plane_bytes[:, tokens])
-            hq = quantize("h_s%d" % half, hidden[:].rearrange("p n t -> p (n t)"), HALF)
-            tokens = slice(HALF * half, HALF * (half + 1))
-            result = keep.tile([P, HALF], F32, name="result%d" % half)
-            nc.vector.tensor_tensor(out=result[:], in0=down(q2s, hq, HALF), in1=routed[:, tokens], op=ADD)
-            nc.sync.dma_start(out=out[:, tokens], in_=result[:])
+        for step in ORDER:
+            if step == "gw":
+                nc.vector.tensor_copy(slot_words[:], words[:].bitcast(U32).indirect(offsets[:]))
+            elif step == "gs":
+                nc.vector.tensor_copy(slot_planes[:], plane_bytes.indirect(offsets[:]))
+            elif step.startswith("cS_") or step.startswith("cV_"):
+                cast_up(step[3:], step[1] == "S")
+            elif step.startswith("c_"):
+                cast_down(step[2:])
+            elif step.startswith("q_w2"):
+                quantize(step[2:], staged[step[2:]][:].rearrange("p c i j -> p (c i j)"), N)
+            elif step.startswith("q_"):
+                quantize(step[2:], staged[step[2:]][:].rearrange("p u t m j -> p (u t m j)"), H)
+            elif step.startswith("qh"):
+                quantize(step[1:], hidden[step[2:]][:].rearrange("p n t -> p (n t)"), hidden[step[2:]].shape[1])
+            elif step.startswith("m2"):
+                down(step[2:])
+            elif step.startswith("m"):
+                up(step[1], step[2:])
+            elif step.startswith("g"):
+                activate(step[1:])
+            elif step.startswith("h"):
+                gated(step[1:])
+            elif step.startswith("y"):
+                ys[step[1]] = keep.tile([P, C], F32, name="y_" + step[1])
+                nc.scalar.copy(out=ys[step[1]][:], in_=banks["2" + step[1]])
+            elif step.startswith("sc"):
+                e = int(step[2])
+                nc.vector.tensor_tensor(routed[:].indirect(offsets[:, 8 * e : 8 * (e + 1)]), ys[step[2]][:], gates[:, C * e : C * (e + 1)], MULT)
+            elif step.startswith("add"):
+                tokens = slice(GROUP * CHUNK * int(step[3]), GROUP * CHUNK * (int(step[3]) + 1))
+                result = keep.tile([P, GROUP * CHUNK], F32, name="result" + step[3])
+                nc.vector.tensor_tensor(out=result[:], in0=banks["2s" + step[3]], in1=routed[:, tokens], op=ADD)
+                nc.sync.dma_start(out=out[:, tokens], in_=result[:])

@@ -23,10 +23,10 @@ P = 128
 PACK = 4
 CHUNK = 128
 HALF = 512
-LOADS = ["w1sa","w1sb","w11","offs","x","w3s","w10","w30","w31","w12","w21","w32","gate","w13","w33b","w33a","w20","w22","w23","w2s"]
-SPLIT = {"w1s":64,"w3s":0,"w10":16,"w30":112,"w11":112,"w31":80,"w12":88,"w32":128,"w13":88,"w33":64}
-DOWN_ON = {"0":"S","1":"S","2":"S","3":"V","s":"S"}
-ORDER = ["cS_w11","gw","cV_w1s","cS_w1s","cS_w31","cV_w3s","q_w1s","gs","cV_w11","q_w11","cV_w31","cV_w30","q_w31","m1s5","gs5","m1s2","cV_w10","cS_w30","gs2","m1s1","q_w3s","cS_w10","m1s0","c_w22","q_w30","m3s5","hs5","c_w21","m3s2","m1s3","gs0","cS_w13","gs1","hs2","cV_w13","cS_w12","q_w10","m3s0","m3s1","q_w13","gs3","m1s7","q_w22","hs0","c_w23","m1s6","c_w20","cS_w33","cV_w12","c_w2s","q_w12","m11","cV_w33","gs7","m10","g1","hs1","m3s3","q_w23","m31","gs6","h1","m3s7","hs3","hs7","cS_w32","qh1","m30","m12","m3s6","q_w20","m3s4","g0","hs6","q_w21","m21","q_w33","m13","g3","h0","g2","qh0","m1s4","q_w32","gs4","m33","h3","qhs0","y1","m20","m32","h2","hs4","qh3","sc1","y0","qh2","m22","sc0","m23","q_w2s","y2","sc2","y3","sc3","qhs1","m2s1","m2s0","add0","add1"]
+LOADS = ["w1sa","offs","w1sb","x","w20","w3s","w31","w11","w12","w30","w32","w10","w13","w33a","w22","w33b","w21","w2s","w23","gate"]
+SPLIT = {"w1s":64,"w3s":16,"w11":88,"w31":56,"w12":128,"w32":104,"w10":0,"w30":128,"w13":64,"w33":64}
+DOWN_ON = {"0":"S","1":"S","2":"S","3":"S","s":"S"}
+ORDER = ["cS_w1s","cV_w1s","cS_w3s","cV_w3s","q_w1s","cS_w31","cV_w31","cS_w11","cV_w11","cS_w12","c_w20","q_w3s","m1s0","gs0","gw","gs","q_w31","m1s1","gs1","m3s0","hs0","cV_w10","m1s2","gs2","q_w11","m1s3","gs3","m3s1","hs1","cS_w30","c_w21","q_w12","q_w10","m1s4","gs4","q_w21","m1s5","gs5","m3s2","hs2","cS_w32","cV_w32","q_w30","cS_w13","cV_w13","c_w2s","m1s6","gs6","q_w20","m3s3","hs3","q_w13","m11","g1","q_w2s","m1s7","gs7","m3s4","hs4","m3s5","hs5","m31","h1","m3s6","hs6","m3s7","hs7","qhs1","q_w32","m10","g0","m30","h0","qh1","m12","g2","qh0","cS_w33","cV_w33","m20","y0","sc0","c_w22","m32","h2","qh2","q_w33","m21","y1","sc1","m13","g3","c_w23","q_w22","m22","y2","sc2","m33","h3","qh3","qhs0","q_w23","m23","y3","sc3","m2s0","add0","m2s1","add1"]
 GROUP = 4
 
 
@@ -45,12 +45,12 @@ def tile_moe_shr_glu_gelu_kernel(tc, x_words, x_scales, w1, w3, w2, gate, offs, 
         slot_words = keep.tile([P, SLOTS], U32, name="slot_words", align_bytes=64)
         slot_planes = keep.tile([P, SLOTS], U8, name="slot_planes", align_bytes=64)
         plane_bytes = planes[:].bitcast(U8)
-        nc.vector.memset(planes[:], 0)
-        nc.vector.memset(routed[:], 0.0)
         warm = keep.tile([P, 2], F32, name="warm")
         nc.vector.memset(warm[:, 0:1], 0.0)
         nc.scalar.activation(out=warm[:, 1:2], in_=warm[:, 0:1], func=GELU)
 
+        nc.vector.memset(planes[:], 0)
+        nc.vector.memset(routed[:], 0.0)
         for q in range(4):
             nc.scalar.dma_start(out=planes[32 * q : 32 * q + 4, :], in_=x_scales[0, 4 * q : 4 * q + 4, :].bitcast(I32))
         raw = {}
@@ -65,7 +65,8 @@ def tile_moe_shr_glu_gelu_kernel(tc, x_words, x_scales, w1, w3, w2, gate, offs, 
             else:
                 src = mats[name[:2]]["0123s".index(name[2])].rearrange("(p j) c -> p j c", j=PACK)
                 if len(name) == 4:
-                    src = src[:, :, 0:256] if name[3] == "a" else src[:, :, 256:512]
+                    cut = PACK * SPLIT[name[:3]]
+                    src = src[:, :, 0:cut] if name[3] == "a" else src[:, :, cut:H]
                 raw[name] = keep.tile(list(src.shape), F32, name="raw_" + name)
                 nc.sync.dma_start(out=raw[name][:], in_=src)
 
@@ -91,6 +92,9 @@ def tile_moe_shr_glu_gelu_kernel(tc, x_words, x_scales, w1, w3, w2, gate, offs, 
 
         def cast_down(name):
             staged[name] = ring.tile([P, N // 4, 4, PACK], BF16, name="staged_down", align_bytes=64)
+            if DOWN_ON[name[2]] == "G":
+                nc.gpsimd.tensor_copy(out=staged[name][:].rearrange("p c i j -> p (c i) j"), in_=raw[name][:].rearrange("p j n -> p n j"))
+                return
             copy = nc.scalar.copy if DOWN_ON[name[2]] == "S" else nc.vector.tensor_copy
             copy(out=staged[name][:].rearrange("p c i j -> p c j i"), in_=raw[name][:].rearrange("p j (c i) -> p c j i", i=4))
 

@@ -23,10 +23,10 @@ P = 128
 PACK = 4
 CHUNK = 128
 HALF = 512
-LOADS = ["w1sa","offs","w1sb","x","w20","w3s","w31","w11","w12","w30","w32","w10","w13","w33a","w22","w33b","w21","w2s","w23","gate"]
-SPLIT = {"w1s":64,"w3s":16,"w11":88,"w31":56,"w12":128,"w32":104,"w10":0,"w30":128,"w13":64,"w33":64}
-DOWN_ON = {"0":"S","1":"S","2":"S","3":"S","s":"S"}
-ORDER = ["cS_w1s","cV_w1s","cS_w3s","cV_w3s","q_w1s","cS_w31","cV_w31","cS_w11","cV_w11","cS_w12","c_w20","q_w3s","m1s0","gs0","gw","gs","q_w31","m1s1","gs1","m3s0","hs0","cV_w10","m1s2","gs2","q_w11","m1s3","gs3","m3s1","hs1","cS_w30","c_w21","q_w12","q_w10","m1s4","gs4","q_w21","m1s5","gs5","m3s2","hs2","cS_w32","cV_w32","q_w30","cS_w13","cV_w13","c_w2s","m1s6","gs6","q_w20","m3s3","hs3","q_w13","m11","g1","q_w2s","m1s7","gs7","m3s4","hs4","m3s5","hs5","m31","h1","m3s6","hs6","m3s7","hs7","qhs1","q_w32","m10","g0","m30","h0","qh1","m12","g2","qh0","cS_w33","cV_w33","m20","y0","sc0","c_w22","m32","h2","qh2","q_w33","m21","y1","sc1","m13","g3","c_w23","q_w22","m22","y2","sc2","m33","h3","qh3","qhs0","q_w23","m23","y3","sc3","m2s0","add0","m2s1","add1"]
+LOADS = ["w1sb","offs","w1sa","w3s","x","w11","w31","w30","w12","w20","w22","w10","w32","w33b","w13","w23","w33a","w21","w2s","gate"]
+SPLIT = {"w1s":64,"w3s":112,"w11":80,"w31":128,"w12":64,"w32":112,"w10":128,"w30":80,"w13":80,"w33":64}
+DOWN_ON = {"0":"V","1":"S","2":"S","3":"S","s":"S"}
+ORDER = ["cV_w1s","cS_w1s","q_w1s","cS_w3s","cV_w3s","gw","gs","m1s0","gs0","q_w3s","m1s1","gs1","m3s0","hs0","m1s2","gs2","m1s3","gs3","cS_w11","cV_w11","m3s1","hs1","m1s4","gs4","m3s2","hs2","m3s3","hs3","m1s5","gs5","q_w11","cS_w31","m3s4","hs4","m1s6","gs6","qhs0","m1s7","gs7","m3s5","hs5","q_w31","m3s6","hs6","m3s7","hs7","cS_w12","cV_w12","c_w22","c_w20","q_w22","cS_w30","cV_w30","q_w12","cS_w10","qhs1","cS_w32","cV_w32","q_w20","q_w30","cV_w33","cS_w33","q_w10","m10","g0","q_w32","m30","h0","m11","g1","m12","g2","m31","h1","m32","h2","cS_w13","cV_w13","qh0","q_w13","c_w21","qh1","qh2","q_w33","m20","y0","sc0","m13","g3","q_w21","m33","h3","m21","y1","sc1","c_w23","m22","y2","sc2","c_w2s","qh3","q_w23","m23","y3","sc3","q_w2s","m2s0","add0","m2s1","add1"]
 GROUP = 4
 
 
@@ -34,7 +34,8 @@ def tile_moe_shr_glu_gelu_kernel(tc, x_words, x_scales, w1, w3, w2, gate, offs, 
     nc = tc.nc
     with ExitStack() as ctx:
         keep = ctx.enter_context(tc.tile_pool(name="keep", bufs=1))
-        ring = ctx.enter_context(tc.tile_pool(name="ring", bufs=4))
+        ring = ctx.enter_context(tc.tile_pool(name="ring", bufs=10))
+        small = ctx.enter_context(tc.tile_pool(name="small", bufs=26))
         psum = ctx.enter_context(tc.psum_pool(name="psum", bufs=1))
 
         offsets = keep.tile([P, SLOTS // 16], U16, name="offsets")
@@ -43,7 +44,6 @@ def tile_moe_shr_glu_gelu_kernel(tc, x_words, x_scales, w1, w3, w2, gate, offs, 
         gates = keep.tile([P, SLOTS], F32, name="gates")
         routed = keep.tile([P, T], F32, name="routed")
         slot_words = keep.tile([P, SLOTS], U32, name="slot_words", align_bytes=64)
-        slot_planes = keep.tile([P, SLOTS], U8, name="slot_planes", align_bytes=64)
         plane_bytes = planes[:].bitcast(U8)
         warm = keep.tile([P, 2], F32, name="warm")
         nc.vector.memset(warm[:, 0:1], 0.0)
@@ -70,28 +70,33 @@ def tile_moe_shr_glu_gelu_kernel(tc, x_words, x_scales, w1, w3, w2, gate, offs, 
                 raw[name] = keep.tile(list(src.shape), F32, name="raw_" + name)
                 nc.sync.dma_start(out=raw[name][:], in_=src)
 
-        staged, quant, banks, acts, hidden, ys = {}, {}, {}, {}, {}, {}
+        staged, quant, banks, acts, hidden, ys, gathered = {}, {}, {}, {}, {}, {}, {}
 
         def quantize(name, src, width):
             codes = keep.tile([P, width], U32, name="codes_" + name, align_bytes=64)
-            scales = keep.tile([P, width], U8, name="scales_" + name, align_bytes=64)
+            scales = small.tile([P, width], U8, name="scales_" + name, tag="small", align_bytes=64)
             nc.vector.quantize_mx(out=codes[:].bitcast(FP8X4), scales=scales[:], in_=src)
             quant[name] = (codes, scales)
 
         def cast_up(name, on_scalar):
             if name not in staged:
-                staged[name] = ring.tile([P, 2, 2, P, PACK], BF16, name="staged_up", align_bytes=64)
+                staged[name] = ring.tile([P, 2, 2, P, PACK], BF16, name="staged_" + name, tag="stage", align_bytes=64)
             split = SPLIT[name]
             if name in raw:
                 src = raw[name][:, :, 0 : PACK * split] if on_scalar else raw[name][:, :, PACK * split : H]
             else:
                 src = raw[name + ("a" if on_scalar else "b")][:]
             dst = staged[name][:, :, :, 0:split, :] if on_scalar else staged[name][:, :, :, split:P, :]
-            copy = nc.scalar.copy if on_scalar else nc.vector.tensor_copy
-            copy(out=dst.rearrange("p u t m j -> p u m j t"), in_=src.rearrange("p j (m u t) -> p u m j t", u=2, t=2))
+            dst = dst.rearrange("p u t m j -> p u m j t")
+            src = src.rearrange("p j (m u t) -> p u m j t", u=2, t=2)
+            if on_scalar:
+                nc.scalar.copy(out=dst, in_=src)
+            else:
+                for u in range(2):
+                    nc.vector.tensor_copy(out=dst[:, u], in_=src[:, u])
 
         def cast_down(name):
-            staged[name] = ring.tile([P, N // 4, 4, PACK], BF16, name="staged_down", align_bytes=64)
+            staged[name] = ring.tile([P, N // 4, 4, PACK], BF16, name="staged_" + name, tag="stage", align_bytes=64)
             if DOWN_ON[name[2]] == "G":
                 nc.gpsimd.tensor_copy(out=staged[name][:].rearrange("p c i j -> p (c i) j"), in_=raw[name][:].rearrange("p j n -> p n j"))
                 return
@@ -105,7 +110,7 @@ def tile_moe_shr_glu_gelu_kernel(tc, x_words, x_scales, w1, w3, w2, gate, offs, 
                 x_codes, x_planes = words[:, tokens], plane_bytes[:, tokens]
             else:
                 tokens = slice(C * int(unit), C * (int(unit) + 1))
-                x_codes, x_planes = slot_words[:, tokens], slot_planes[:, tokens]
+                x_codes, x_planes = slot_words[:, tokens], gathered["planes"][:, tokens]
             bank = psum.tile([P, PACK, CHUNK], F32, name="a" + which, bufs=3)
             for t in range(PACK):
                 cols = slice(P * t, P * (t + 1))
@@ -114,7 +119,7 @@ def tile_moe_shr_glu_gelu_kernel(tc, x_words, x_scales, w1, w3, w2, gate, offs, 
             banks[which + unit] = bank[:].rearrange("p t n -> p n t")
 
         def activate(unit):
-            acts[unit] = keep.tile([P, CHUNK, PACK], F32, name="act_" + unit)
+            acts[unit] = ring.tile([P, CHUNK, PACK], F32, name="act_" + unit, tag="stage", align_bytes=64)
             nc.scalar.activation(out=acts[unit][:], in_=banks["1" + unit], func=GELU)
 
         def gated(unit):
@@ -123,7 +128,9 @@ def tile_moe_shr_glu_gelu_kernel(tc, x_words, x_scales, w1, w3, w2, gate, offs, 
                 key, width = "s%d" % group, GROUP * CHUNK
             else:
                 key, place, width = unit, 0, C
-            if key not in hidden:
+            if unit[0] != "s":
+                hidden[key] = small.tile([P, width, PACK], BF16, name="hidden_" + key, tag="small", align_bytes=64)
+            elif key not in hidden:
                 hidden[key] = keep.tile([P, width, PACK], BF16, name="hidden_" + key, align_bytes=64)
             nc.vector.tensor_tensor(out=hidden[key][:, CHUNK * place : CHUNK * (place + 1), :], in0=banks["3" + unit], in1=acts[unit][:], op=MULT)
 
@@ -139,7 +146,8 @@ def tile_moe_shr_glu_gelu_kernel(tc, x_words, x_scales, w1, w3, w2, gate, offs, 
             if step == "gw":
                 nc.vector.tensor_copy(slot_words[:], words[:].bitcast(U32).indirect(offsets[:]))
             elif step == "gs":
-                nc.vector.tensor_copy(slot_planes[:], plane_bytes.indirect(offsets[:]))
+                gathered["planes"] = small.tile([P, SLOTS], U8, name="slot_planes", tag="small", align_bytes=64)
+                nc.vector.tensor_copy(gathered["planes"][:], plane_bytes.indirect(offsets[:]))
             elif step.startswith("cS_") or step.startswith("cV_"):
                 cast_up(step[3:], step[1] == "S")
             elif step.startswith("c_"):
@@ -159,7 +167,7 @@ def tile_moe_shr_glu_gelu_kernel(tc, x_words, x_scales, w1, w3, w2, gate, offs, 
             elif step.startswith("h"):
                 gated(step[1:])
             elif step.startswith("y"):
-                ys[step[1]] = keep.tile([P, C], F32, name="y_" + step[1])
+                ys[step[1]] = ring.tile([P, C], F32, name="y_" + step[1], tag="stage", align_bytes=64)
                 nc.scalar.copy(out=ys[step[1]][:], in_=banks["2" + step[1]])
             elif step.startswith("sc"):
                 e = int(step[2])

from contextlib import ExitStack

import concourse.mybir as mybir

K, T, E, C, H, N = 512, 1024, 4, 128, 512, 128
SLOTS = E * C
SHARED = E

FLOPS = 2 * (T + SLOTS) * (2 * K * H + H * N)

F32 = mybir.dt.float32
BF16 = mybir.dt.bfloat16
I32 = mybir.dt.int32
U32 = mybir.dt.uint32
U16 = mybir.dt.uint16
U8 = mybir.dt.uint8
FP8X4 = mybir.dt.float8_e4m3fn_x4
GELU = mybir.ActivationFunctionType.Gelu_apprx_tanh
MULT = mybir.AluOpType.mult
ADD = mybir.AluOpType.add

P = 128
PACK = 4
CHUNK = 128
HALF = 512
LOADS = ["w1sb","offs","w1sa","w3s","x","w11","w31","w30","w12","w20","w22","w10","w32","w33b","w13","w23","w33a","w21","w2s","gate"]
SPLIT = {"w1s":64,"w3s":112,"w11":80,"w31":128,"w12":64,"w32":112,"w10":128,"w30":80,"w13":80,"w33":64}
DOWN_ON = {"0":"V","1":"S","2":"S","3":"S","s":"S"}
ORDER = ["cV_w1s","cS_w1s","q_w1s","cS_w3s","cV_w3s","gw","gs","m1s0","gs0","q_w3s","m1s1","gs1","m3s0","hs0","m1s2","gs2","m1s3","gs3","cS_w11","cV_w11","m3s1","hs1","m1s4","gs4","m3s2","hs2","m3s3","hs3","m1s5","gs5","q_w11","cS_w31","m3s4","hs4","m1s6","gs6","qhs0","m1s7","gs7","m3s5","hs5","q_w31","m3s6","hs6","m3s7","hs7","cS_w12","cV_w12","c_w22","c_w20","q_w22","cS_w30","cV_w30","q_w12","cS_w10","qhs1","cS_w32","cV_w32","q_w20","q_w30","cV_w33","cS_w33","q_w10","m10","g0","q_w32","m30","h0","m11","g1","m12","g2","m31","h1","m32","h2","cS_w13","cV_w13","qh0","q_w13","c_w21","qh1","qh2","q_w33","m20","y0","sc0","m13","g3","q_w21","m33","h3","m21","y1","sc1","c_w23","m22","y2","sc2","c_w2s","qh3","q_w23","m23","y3","sc3","q_w2s","m2s0","add0","m2s1","add1"]
GROUP = 4


def tile_moe_shr_glu_gelu_kernel(tc, x_words, x_scales, w1, w3, w2, gate, offs, out):
    nc = tc.nc
    with ExitStack() as ctx:
        keep = ctx.enter_context(tc.tile_pool(name="keep", bufs=1))
        ring = ctx.enter_context(tc.tile_pool(name="ring", bufs=10))
        small = ctx.enter_context(tc.tile_pool(name="small", bufs=26))
        psum = ctx.enter_context(tc.psum_pool(name="psum", bufs=1))

        offsets = keep.tile([P, SLOTS // 16], U16, name="offsets")
        words = keep.tile([P, T], I32, name="words", align_bytes=64)
        planes = keep.tile([P, T // 4], I32, name="planes", align_bytes=64)
        gates = keep.tile([P, SLOTS], F32, name="gates")
        routed = keep.tile([P, T], F32, name="routed")
        slot_words = keep.tile([P, SLOTS], U32, name="slot_words", align_bytes=64)
        plane_bytes = planes[:].bitcast(U8)
        warm = keep.tile([P, 2], F32, name="warm")
        nc.vector.memset(warm[:, 0:1], 0.0)
        nc.scalar.activation(out=warm[:, 1:2], in_=warm[:, 0:1], func=GELU)

        nc.vector.memset(planes[:], 0)
        nc.vector.memset(routed[:], 0.0)
        for q in range(4):
            nc.scalar.dma_start(out=planes[32 * q : 32 * q + 4, :], in_=x_scales[0, 4 * q : 4 * q + 4, :].bitcast(I32))
        raw = {}
        mats = {"w1": w1, "w3": w3, "w2": w2}
        for name in LOADS:
            if name == "x":
                nc.sync.dma_start(out=words[:], in_=x_words[0].rearrange("p t r -> p (t r)").bitcast(I32))
            elif name == "offs":
                nc.sync.dma_start(offsets[:], offs)
            elif name == "gate":
                nc.sync.dma_start(out=gates[:], in_=gate)
            else:
                src = mats[name[:2]]["0123s".index(name[2])].rearrange("(p j) c -> p j c", j=PACK)
                if len(name) == 4:
                    cut = PACK * SPLIT[name[:3]]
                    src = src[:, :, 0:cut] if name[3] == "a" else src[:, :, cut:H]
                raw[name] = keep.tile(list(src.shape), F32, name="raw_" + name)
                nc.sync.dma_start(out=raw[name][:], in_=src)

        staged, quant, banks, acts, hidden, ys, gathered = {}, {}, {}, {}, {}, {}, {}

        def quantize(name, src, width):
            codes = keep.tile([P, width], U32, name="codes_" + name, align_bytes=64)
            scales = small.tile([P, width], U8, name="scales_" + name, tag="small", align_bytes=64)
            nc.vector.quantize_mx(out=codes[:].bitcast(FP8X4), scales=scales[:], in_=src)
            quant[name] = (codes, scales)

        def cast_up(name, on_scalar):
            if name not in staged:
                staged[name] = ring.tile([P, 2, 2, P, PACK], BF16, name="staged_" + name, tag="stage", align_bytes=64)
            split = SPLIT[name]
            if name in raw:
                src = raw[name][:, :, 0 : PACK * split] if on_scalar else raw[name][:, :, PACK * split : H]
            else:
                src = raw[name + ("a" if on_scalar else "b")][:]
            dst = staged[name][:, :, :, 0:split, :] if on_scalar else staged[name][:, :, :, split:P, :]
            dst = dst.rearrange("p u t m j -> p u m j t")
            src = src.rearrange("p j (m u t) -> p u m j t", u=2, t=2)
            if on_scalar:
                nc.scalar.copy(out=dst, in_=src)
            else:
                for u in range(2):
                    nc.vector.tensor_copy(out=dst[:, u], in_=src[:, u])

        def cast_down(name):
            staged[name] = ring.tile([P, N // 4, 4, PACK], BF16, name="staged_" + name, tag="stage", align_bytes=64)
            if DOWN_ON[name[2]] == "G":
                nc.gpsimd.tensor_copy(out=staged[name][:].rearrange("p c i j -> p (c i) j"), in_=raw[name][:].rearrange("p j n -> p n j"))
                return
            copy = nc.scalar.copy if DOWN_ON[name[2]] == "S" else nc.vector.tensor_copy
            copy(out=staged[name][:].rearrange("p c i j -> p c j i"), in_=raw[name][:].rearrange("p j (c i) -> p c j i", i=4))

        def up(which, unit):
            codes, scales = quant["w" + which + unit[0]]
            if unit[0] == "s":
                tokens = slice(CHUNK * int(unit[1]), CHUNK * (int(unit[1]) + 1))
                x_codes, x_planes = words[:, tokens], plane_bytes[:, tokens]
            else:
                tokens = slice(C * int(unit), C * (int(unit) + 1))
                x_codes, x_planes = slot_words[:, tokens], gathered["planes"][:, tokens]
            bank = psum.tile([P, PACK, CHUNK], F32, name="a" + which, bufs=3)
            for t in range(PACK):
                cols = slice(P * t, P * (t + 1))
                nc.tensor.matmul_mx(out=bank[:, t, :], lhsT=codes[:, cols].bitcast(FP8X4), lhsT_scale=scales[:, cols],
                                    rhs=x_codes.bitcast(FP8X4), rhs_scale=x_planes, start=True, stop=True)
            banks[which + unit] = bank[:].rearrange("p t n -> p n t")

        def activate(unit):
            acts[unit] = ring.tile([P, CHUNK, PACK], F32, name="act_" + unit, tag="stage", align_bytes=64)
            nc.scalar.activation(out=acts[unit][:], in_=banks["1" + unit], func=GELU)

        def gated(unit):
            if unit[0] == "s":
                group, place = divmod(int(unit[1]), GROUP)
                key, width = "s%d" % group, GROUP * CHUNK
            else:
                key, place, width = unit, 0, C
            if unit[0] != "s":
                hidden[key] = small.tile([P, width, PACK], BF16, name="hidden_" + key, tag="small", align_bytes=64)
            elif key not in hidden:
                hidden[key] = keep.tile([P, width, PACK], BF16, name="hidden_" + key, align_bytes=64)
            nc.vector.tensor_tensor(out=hidden[key][:, CHUNK * place : CHUNK * (place + 1), :], in0=banks["3" + unit], in1=acts[unit][:], op=MULT)

        def down(key):
            width = GROUP * CHUNK if key[0] == "s" else C
            bank = psum.tile([P, HALF], F32, name="y", bufs=2)
            wq, hq = quant["w2" + key[0]], quant["h" + key]
            nc.tensor.matmul_mx(out=bank[:, 0:width], lhsT=wq[0][:].bitcast(FP8X4), lhsT_scale=wq[1][:],
                                rhs=hq[0][:].bitcast(FP8X4), rhs_scale=hq[1][:], start=True, stop=True)
            banks["2" + key] = bank[:, 0:width]

        for step in ORDER:
            if step == "gw":
                nc.vector.tensor_copy(slot_words[:], words[:].bitcast(U32).indirect(offsets[:]))
            elif step == "gs":
                gathered["planes"] = small.tile([P, SLOTS], U8, name="slot_planes", tag="small", align_bytes=64)
                nc.vector.tensor_copy(gathered["planes"][:], plane_bytes.indirect(offsets[:]))
            elif step.startswith("cS_") or step.startswith("cV_"):
                cast_up(step[3:], step[1] == "S")
            elif step.startswith("c_"):
                cast_down(step[2:])
            elif step.startswith("q_w2"):
                quantize(step[2:], staged[step[2:]][:].rearrange("p c i j -> p (c i j)"), N)
            elif step.startswith("q_"):
                quantize(step[2:], staged[step[2:]][:].rearrange("p u t m j -> p (u t m j)"), H)
            elif step.startswith("qh"):
                quantize(step[1:], hidden[step[2:]][:].rearrange("p n t -> p (n t)"), hidden[step[2:]].shape[1])
            elif step.startswith("m2"):
                down(step[2:])
            elif step.startswith("m"):
                up(step[1], step[2:])
            elif step.startswith("g"):
                activate(step[1:])
            elif step.startswith("h"):
                gated(step[1:])
            elif step.startswith("y"):
                ys[step[1]] = ring.tile([P, C], F32, name="y_" + step[1], tag="stage", align_bytes=64)
                nc.scalar.copy(out=ys[step[1]][:], in_=banks["2" + step[1]])
            elif step.startswith("sc"):
                e = int(step[2])
                nc.vector.tensor_tensor(routed[:].indirect(offsets[:, 8 * e : 8 * (e + 1)]), ys[step[2]][:], gates[:, C * e : C * (e + 1)], MULT)
            elif step.startswith("add"):
                tokens = slice(GROUP * CHUNK * int(step[3]), GROUP * CHUNK * (int(step[3]) + 1))
                result = keep.tile([P, GROUP * CHUNK], F32, name="result" + step[3])
                nc.vector.tensor_tensor(out=result[:], in0=banks["2s" + step[3]], in1=routed[:, tokens], op=ADD)
                nc.sync.dma_start(out=out[:, tokens], in_=result[:])
